import numpy as np
import ml_dtypes


def mxq(x, axis, fmt="e4m3"):
    dtype, down = {"e4m3": (ml_dtypes.float8_e4m3fn, 7), "e5m2": (ml_dtypes.float8_e5m2, 14)}[fmt]
    v = np.moveaxis(np.asarray(x, np.float32).astype(ml_dtypes.bfloat16).astype(np.float64), axis, -1)
    blocks = v.reshape(v.shape[:-1] + (-1, 32))
    amax = np.abs(blocks).max(-1, keepdims=True)
    byte = np.maximum(np.where(amax > 0, np.frexp(amax)[1] - 1 + 127, 0) - down, 1)
    scale = np.exp2(byte - 127.0)
    codes = (blocks / scale).astype(np.float32).astype(dtype).astype(np.float64)
    return np.moveaxis((codes * scale).reshape(v.shape), -1, axis)


WIDE = False


def mx_kscale(k, group=512):
    if not WIDE:
        return np.ones(k)
    levels = np.array([18, -18])
    if group != 512:
        return np.exp2(np.random.permutation(np.resize(levels, k // group))).repeat(group)
    if k % 512:
        return np.exp2(np.random.permutation(np.resize(levels, k // 32))).repeat(32)
    a = np.empty((k // 512, 16))
    for p in range(k // 512):
        a[p, :8] = np.random.permutation(np.resize(levels, 8))
        for g in range(8):
            far = levels[np.abs(levels - a[p, g]) >= 10]
            a[p, g + 8] = far[np.random.randint(len(far))]
    return np.exp2(a.ravel()).repeat(32)


def f64(x):
    return np.asarray(x).astype(np.float64)


def silu(v):
    return v / (1.0 + np.exp(-v))


G, D, M, N = 4, 128, 128, 512


def setup_inputs():
    n = np.random.standard_normal
    s = mx_kscale(D, 0)[:, None]
    return {
        "x": (n((G, D, N)) * s).astype(np.float32),
        "w": (n((G, D, M)) / np.sqrt(D) / s).astype(np.float32),
        "u": (n((G, D, M)) / np.sqrt(D) / s).astype(np.float32),
    }


def reference(x, w, u):
    xq = mxq(f64(x), 1, "e4m3")
    h = mxq(f64(w), 1, "e4m3").transpose(0, 2, 1) @ xq
    g = mxq(f64(u), 1, "e4m3").transpose(0, 2, 1) @ xq
    y = silu(h) * g
    return y

@@ -1,0 +1,96 @@
+from contextlib import ExitStack
+
+import concourse.mybir as mybir
+
+G, D, M, N = 4, 128, 128, 512
+FLOPS = 2 * 2 * G * D * M * N
+
+F32 = mybir.dt.float32
+BF16 = mybir.dt.bfloat16
+U32 = mybir.dt.uint32
+U8 = mybir.dt.uint8
+FP8X4 = mybir.dt.float8_e4m3fn_x4
+SILU = mybir.ActivationFunctionType.Silu
+MULT = mybir.AluOpType.mult
+
+P = 128
+PACK = 4
+ROWS = D // PACK
+HALF = N // 2
+RUN = 4
+VEC_COLS = 176
+
+
+def interleave(copy, dst, src, lo, hi):
+    copy(
+        out=dst[:, PACK * lo : PACK * hi].rearrange("p (c i j) -> p c j i", i=RUN, j=PACK),
+        in_=src[:, :, lo:hi].rearrange("p j (c i) -> p c j i", i=RUN),
+    )
+
+
+def tile_rows_gglu_silu_kernel(tc, x, w, u, out):
+    nc = tc.nc
+    x_rows = x.rearrange("g (p j) n -> (g p) j n", j=PACK)
+    w_rows = w.rearrange("g (p j) m -> (g p) j m", j=PACK)
+    u_rows = u.rearrange("g (p j) m -> (g p) j m", j=PACK)
+
+    with ExitStack() as ctx:
+        sb = ctx.enter_context(tc.tile_pool(name="sb", bufs=1))
+        ps = ctx.enter_context(tc.psum_pool(name="ps", bufs=1))
+        ctx.enter_context(tc.manual_schedule())
+
+        w_raw = sb.tile([P, PACK, M], F32, name="w_raw")
+        u_raw = sb.tile([P, PACK, M], F32, name="u_raw")
+        x_raw = [sb.tile([P, PACK, HALF], F32, name="x_raw%d" % c) for c in range(2)]
+        w_bf = sb.tile([P, PACK * M], BF16, name="w_bf", align_bytes=64)
+        u_bf = sb.tile([P, PACK * M], BF16, name="u_bf", align_bytes=64)
+        x_bf = [sb.tile([P, PACK * HALF], BF16, name="x_bf%d" % c, align_bytes=64) for c in range(2)]
+        w_codes = sb.tile([P, M], U32, name="w_codes", align_bytes=64)
+        w_scales = sb.tile([P, M], U8, name="w_scales", align_bytes=64)
+        u_codes = sb.tile([P, M], U32, name="u_codes", align_bytes=64)
+        u_scales = sb.tile([P, M], U8, name="u_scales", align_bytes=64)
+        x_codes = sb.tile([P, N], U32, name="x_codes", align_bytes=64)
+        x_scales = sb.tile([P, N], U8, name="x_scales", align_bytes=64)
+        warm = sb.tile([P, 1], F32, name="warm")
+        z_ps = [ps.tile([M, N], F32, name="z_ps%d" % g) for g in range(G)]
+        v_ps = [ps.tile([M, N], F32, name="v_ps%d" % g) for g in range(G)]
+        act = [sb.tile([M, N], F32, name="act%d" % g) for g in range(G)]
+        res = [sb.tile([M, N], F32, name="res%d" % g) for g in range(G)]
+
+        nc.sync.dma_start(out=w_raw[:], in_=w_rows)
+        nc.sync.dma_start(out=x_raw[0][:], in_=x_rows[:, :, 0:HALF])
+        nc.sync.dma_start(out=x_raw[1][:], in_=x_rows[:, :, HALF:N])
+        nc.sync.dma_start(out=u_raw[:], in_=u_rows)
+
+        def quantize(codes, scales, src):
+            nc.vector.quantize_mx(out=codes.bitcast(FP8X4), scales=scales, in_=src)
+
+        nc.scalar.activation(out=warm[:], in_=w_raw[:, 0, 0:1], func=SILU)
+
+        interleave(nc.vector.tensor_copy, w_bf, w_raw, 0, M)
+        quantize(w_codes[:], w_scales[:], w_bf[:])
+        for c in range(2):
+            cols = slice(c * HALF, (c + 1) * HALF)
+            interleave(nc.vector.tensor_copy, x_bf[c], x_raw[c], 0, VEC_COLS)
+            interleave(nc.scalar.copy, x_bf[c], x_raw[c], VEC_COLS, HALF)
+            quantize(x_codes[:, cols], x_scales[:, cols], x_bf[c][:])
+        interleave(nc.scalar.copy, u_bf, u_raw, 0, M)
+        quantize(u_codes[:], u_scales[:], u_bf[:])
+
+        for banks, codes, scales in ((z_ps, w_codes, w_scales), (v_ps, u_codes, u_scales)):
+            for g in range(G):
+                rows = slice(g * ROWS, (g + 1) * ROWS)
+                nc.tensor.matmul_mx(
+                    out=banks[g][:],
+                    lhsT=codes[rows, :].bitcast(FP8X4),
+                    lhsT_scale=scales[rows, :],
+                    rhs=x_codes[rows, :].bitcast(FP8X4),
+                    rhs_scale=x_scales[rows, :],
+                    start=True,
+                    stop=True,
+                )
+
+        for g in range(G):
+            nc.scalar.activation(out=act[g][:], in_=z_ps[g][:], func=SILU)
+            nc.vector.tensor_tensor(out=res[g][:], in0=v_ps[g][:], in1=act[g][:], op=MULT)
+            nc.sync.dma_start(out=out[g], in_=res[g][:])

@@ -18,6 +18,7 @@ PACK = 4
 ROWS = D // PACK
 HALF = N // 2
 RUN = 4
+N_PASS = 128
 VEC_COLS = 176
 
 
@@ -54,43 +55,68 @@ def tile_rows_gglu_silu_kernel(tc, x, w, u, out):
         warm = sb.tile([P, 1], F32, name="warm")
         z_ps = [ps.tile([M, N], F32, name="z_ps%d" % g) for g in range(G)]
         v_ps = [ps.tile([M, N], F32, name="v_ps%d" % g) for g in range(G)]
-        act = [sb.tile([M, N], F32, name="act%d" % g) for g in range(G)]
-        res = [sb.tile([M, N], F32, name="res%d" % g) for g in range(G)]
+        act = [[sb.tile([M, HALF], F32, name="act%d_%d" % (c, g)) for g in range(G)] for c in range(2)]
+        res = [[sb.tile([M, HALF], F32, name="res%d_%d" % (c, g)) for g in range(G)] for c in range(2)]
 
         nc.sync.dma_start(out=w_raw[:], in_=w_rows)
         nc.sync.dma_start(out=x_raw[0][:], in_=x_rows[:, :, 0:HALF])
-        nc.sync.dma_start(out=x_raw[1][:], in_=x_rows[:, :, HALF:N])
         nc.sync.dma_start(out=u_raw[:], in_=u_rows)
+        nc.sync.dma_start(out=x_raw[1][:], in_=x_rows[:, :, HALF:N])
 
         def quantize(codes, scales, src):
             nc.vector.quantize_mx(out=codes.bitcast(FP8X4), scales=scales, in_=src)
+
+        def quantize_x(c):
+            cols = slice(c * HALF, (c + 1) * HALF)
+            quantize(x_codes[:, cols], x_scales[:, cols], x_bf[c][:])
+
+        def product(banks, codes, scales, c):
+            for n0 in range(c * HALF, (c + 1) * HALF, N_PASS):
+                cols = slice(n0, n0 + N_PASS)
+                for g in range(G):
+                    rows = slice(g * ROWS, (g + 1) * ROWS)
+                    nc.tensor.matmul_mx(
+                        out=banks[g][:, cols],
+                        lhsT=codes[rows, :].bitcast(FP8X4),
+                        lhsT_scale=scales[rows, :],
+                        rhs=x_codes[rows, cols].bitcast(FP8X4),
+                        rhs_scale=x_scales[rows, cols],
+                        start=True,
+                        stop=True,
+                    )
+
+        def activate(c, g):
+            cols = slice(c * HALF, (c + 1) * HALF)
+            nc.scalar.activation(out=act[c][g][:], in_=z_ps[g][:, cols], func=SILU)
+
+        def gate_and_store(c, g):
+            cols = slice(c * HALF, (c + 1) * HALF)
+            nc.vector.tensor_tensor(out=res[c][g][:], in0=v_ps[g][:, cols], in1=act[c][g][:], op=MULT)
+            nc.sync.dma_start(out=out[g, :, cols], in_=res[c][g][:])
 
         nc.scalar.activation(out=warm[:], in_=w_raw[:, 0, 0:1], func=SILU)
 
         interleave(nc.vector.tensor_copy, w_bf, w_raw, 0, M)
         quantize(w_codes[:], w_scales[:], w_bf[:])
-        for c in range(2):
-            cols = slice(c * HALF, (c + 1) * HALF)
-            interleave(nc.vector.tensor_copy, x_bf[c], x_raw[c], 0, VEC_COLS)
-            interleave(nc.scalar.copy, x_bf[c], x_raw[c], VEC_COLS, HALF)
-            quantize(x_codes[:, cols], x_scales[:, cols], x_bf[c][:])
+        interleave(nc.vector.tensor_copy, x_bf[0], x_raw[0], 0, VEC_COLS)
+        interleave(nc.scalar.copy, x_bf[0], x_raw[0], VEC_COLS, HALF)
+        quantize_x(0)
+        product(z_ps, w_codes, w_scales, 0)
         interleave(nc.scalar.copy, u_bf, u_raw, 0, M)
         quantize(u_codes[:], u_scales[:], u_bf[:])
+        product(v_ps, u_codes, u_scales, 0)
 
-        for banks, codes, scales in ((z_ps, w_codes, w_scales), (v_ps, u_codes, u_scales)):
-            for g in range(G):
-                rows = slice(g * ROWS, (g + 1) * ROWS)
-                nc.tensor.matmul_mx(
-                    out=banks[g][:],
-                    lhsT=codes[rows, :].bitcast(FP8X4),
-                    lhsT_scale=scales[rows, :],
-                    rhs=x_codes[rows, :].bitcast(FP8X4),
-                    rhs_scale=x_scales[rows, :],
-                    start=True,
-                    stop=True,
-                )
-
+        activate(0, 0)
+        interleave(nc.vector.tensor_copy, x_bf[1], x_raw[1], 0, VEC_COLS)
+        interleave(nc.scalar.copy, x_bf[1], x_raw[1], VEC_COLS, HALF)
+        gate_and_store(0, 0)
+        quantize_x(1)
+        for g in range(1, G):
+            activate(0, g)
+        product(z_ps, w_codes, w_scales, 1)
+        for g in range(1, G):
+            gate_and_store(0, g)
+        product(v_ps, u_codes, u_scales, 1)
         for g in range(G):
-            nc.scalar.activation(out=act[g][:], in_=z_ps[g][:], func=SILU)
-            nc.vector.tensor_tensor(out=res[g][:], in0=v_ps[g][:], in1=act[g][:], op=MULT)
-            nc.sync.dma_start(out=out[g], in_=res[g][:])
+            activate(1, g)
+            gate_and_store(1, g)

@@ -16,10 +16,14 @@ MULT = mybir.AluOpType.mult
 P = 128
 PACK = 4
 ROWS = D // PACK
-HALF = N // 2
 RUN = 4
 N_PASS = 128
-VEC_COLS = 176
+CHUNKS = (slice(0, 256), slice(256, 384), slice(384, 512))
+STORE_COLS = 256
+
+
+def width(cols):
+    return cols.stop - cols.start
 
 
 def interleave(copy, dst, src, lo, hi):
@@ -34,6 +38,7 @@ def tile_rows_gglu_silu_kernel(tc, x, w, u, out):
     x_rows = x.rearrange("g (p j) n -> (g p) j n", j=PACK)
     w_rows = w.rearrange("g (p j) m -> (g p) j m", j=PACK)
     u_rows = u.rearrange("g (p j) m -> (g p) j m", j=PACK)
+    out_rows = out.rearrange("g m n -> m g n")
 
     with ExitStack() as ctx:
         sb = ctx.enter_context(tc.tile_pool(name="sb", bufs=1))
@@ -42,10 +47,13 @@ def tile_rows_gglu_silu_kernel(tc, x, w, u, out):
 
         w_raw = sb.tile([P, PACK, M], F32, name="w_raw")
         u_raw = sb.tile([P, PACK, M], F32, name="u_raw")
-        x_raw = [sb.tile([P, PACK, HALF], F32, name="x_raw%d" % c) for c in range(2)]
+        x_raw = [sb.tile([P, PACK, width(cols)], F32, name="x_raw%d" % c) for c, cols in enumerate(CHUNKS)]
         w_bf = sb.tile([P, PACK * M], BF16, name="w_bf", align_bytes=64)
         u_bf = sb.tile([P, PACK * M], BF16, name="u_bf", align_bytes=64)
-        x_bf = [sb.tile([P, PACK * HALF], BF16, name="x_bf%d" % c, align_bytes=64) for c in range(2)]
+        x_bf = [
+            sb.tile([P, PACK * width(cols)], BF16, name="x_bf%d" % c, align_bytes=64)
+            for c, cols in enumerate(CHUNKS)
+        ]
         w_codes = sb.tile([P, M], U32, name="w_codes", align_bytes=64)
         w_scales = sb.tile([P, M], U8, name="w_scales", align_bytes=64)
         u_codes = sb.tile([P, M], U32, name="u_codes", align_bytes=64)
@@ -55,23 +63,24 @@ def tile_rows_gglu_silu_kernel(tc, x, w, u, out):
         warm = sb.tile([P, 1], F32, name="warm")
         z_ps = [ps.tile([M, N], F32, name="z_ps%d" % g) for g in range(G)]
         v_ps = [ps.tile([M, N], F32, name="v_ps%d" % g) for g in range(G)]
-        act = [[sb.tile([M, HALF], F32, name="act%d_%d" % (c, g)) for g in range(G)] for c in range(2)]
-        res = [[sb.tile([M, HALF], F32, name="res%d_%d" % (c, g)) for g in range(G)] for c in range(2)]
+        act = [sb.tile([M, G * width(cols)], F32, name="act%d" % c) for c, cols in enumerate(CHUNKS)]
+        res = [sb.tile([M, G * width(cols)], F32, name="res%d" % c) for c, cols in enumerate(CHUNKS)]
 
-        nc.sync.dma_start(out=w_raw[:], in_=w_rows)
-        nc.sync.dma_start(out=x_raw[0][:], in_=x_rows[:, :, 0:HALF])
-        nc.sync.dma_start(out=u_raw[:], in_=u_rows)
-        nc.sync.dma_start(out=x_raw[1][:], in_=x_rows[:, :, HALF:N])
+        def load_x(c):
+            nc.sync.dma_start(out=x_raw[c][:], in_=x_rows[:, :, CHUNKS[c]])
+
+        def interleave_shared(dst, src, vec_cols):
+            interleave(nc.vector.tensor_copy, dst, src, 0, vec_cols)
+            interleave(nc.scalar.copy, dst, src, vec_cols, src.shape[2])
 
         def quantize(codes, scales, src):
             nc.vector.quantize_mx(out=codes.bitcast(FP8X4), scales=scales, in_=src)
 
         def quantize_x(c):
-            cols = slice(c * HALF, (c + 1) * HALF)
-            quantize(x_codes[:, cols], x_scales[:, cols], x_bf[c][:])
+            quantize(x_codes[:, CHUNKS[c]], x_scales[:, CHUNKS[c]], x_bf[c][:])
 
         def product(banks, codes, scales, c):
-            for n0 in range(c * HALF, (c + 1) * HALF, N_PASS):
+            for n0 in range(CHUNKS[c].start, CHUNKS[c].stop, N_PASS):
                 cols = slice(n0, n0 + N_PASS)
                 for g in range(G):
                     rows = slice(g * ROWS, (g + 1) * ROWS)
@@ -85,38 +94,59 @@ def tile_rows_gglu_silu_kernel(tc, x, w, u, out):
                         stop=True,
                     )
 
-        def activate(c, g):
-            cols = slice(c * HALF, (c + 1) * HALF)
-            nc.scalar.activation(out=act[c][g][:], in_=z_ps[g][:, cols], func=SILU)
+        def group_cols(c, first, last):
+            return slice(first * width(CHUNKS[c]), (last + 1) * width(CHUNKS[c]))
 
-        def gate_and_store(c, g):
-            cols = slice(c * HALF, (c + 1) * HALF)
-            nc.vector.tensor_tensor(out=res[c][g][:], in0=v_ps[g][:, cols], in1=act[c][g][:], op=MULT)
-            nc.sync.dma_start(out=out[g, :, cols], in_=res[c][g][:])
+        def activate(c):
+            for g in range(G):
+                nc.scalar.activation(out=act[c][:, group_cols(c, g, g)], in_=z_ps[g][:, CHUNKS[c]], func=SILU)
 
-        nc.scalar.activation(out=warm[:], in_=w_raw[:, 0, 0:1], func=SILU)
+        def gate_and_store(c, groups):
+            per_store = STORE_COLS // width(CHUNKS[c])
+            for g in groups:
+                nc.vector.tensor_tensor(
+                    out=res[c][:, group_cols(c, g, g)],
+                    in0=v_ps[g][:, CHUNKS[c]],
+                    in1=act[c][:, group_cols(c, g, g)],
+                    op=MULT,
+                )
+                if (g + 1) % per_store == 0:
+                    first = g + 1 - per_store
+                    nc.sync.dma_start(
+                        out=out_rows[:, first : g + 1, CHUNKS[c]],
+                        in_=res[c][:, group_cols(c, first, g)].rearrange("m (g n) -> m g n", g=per_store),
+                    )
 
-        interleave(nc.vector.tensor_copy, w_bf, w_raw, 0, M)
-        quantize(w_codes[:], w_scales[:], w_bf[:])
-        interleave(nc.vector.tensor_copy, x_bf[0], x_raw[0], 0, VEC_COLS)
-        interleave(nc.scalar.copy, x_bf[0], x_raw[0], VEC_COLS, HALF)
+        load_x(0)
+        nc.sync.dma_start(out=w_raw[:], in_=w_rows)
+        nc.sync.dma_start(out=u_raw[:], in_=u_rows)
+        load_x(1)
+        load_x(2)
+
+        nc.scalar.activation(out=warm[:], in_=x_raw[0][:, 0, 0:1], func=SILU)
+
+        interleave_shared(x_bf[0], x_raw[0], 160)
+        interleave_shared(w_bf, w_raw, 80)
         quantize_x(0)
+        quantize(w_codes[:], w_scales[:], w_bf[:])
         product(z_ps, w_codes, w_scales, 0)
-        interleave(nc.scalar.copy, u_bf, u_raw, 0, M)
+        interleave_shared(u_bf, u_raw, 64)
         quantize(u_codes[:], u_scales[:], u_bf[:])
         product(v_ps, u_codes, u_scales, 0)
+        activate(0)
 
-        activate(0, 0)
-        interleave(nc.vector.tensor_copy, x_bf[1], x_raw[1], 0, VEC_COLS)
-        interleave(nc.scalar.copy, x_bf[1], x_raw[1], VEC_COLS, HALF)
-        gate_and_store(0, 0)
+        interleave(nc.vector.tensor_copy, x_bf[1], x_raw[1], 0, width(CHUNKS[1]))
+        gate_and_store(0, range(1))
         quantize_x(1)
-        for g in range(1, G):
-            activate(0, g)
         product(z_ps, w_codes, w_scales, 1)
-        for g in range(1, G):
-            gate_and_store(0, g)
+        interleave(nc.scalar.copy, x_bf[2], x_raw[2], 0, width(CHUNKS[2]))
+        gate_and_store(0, range(1, G))
         product(v_ps, u_codes, u_scales, 1)
-        for g in range(G):
-            activate(1, g)
-            gate_and_store(1, g)
+        activate(1)
+
+        quantize_x(2)
+        product(z_ps, w_codes, w_scales, 2)
+        gate_and_store(1, range(G))
+        product(v_ps, u_codes, u_scales, 2)
+        activate(2)
+        gate_and_store(2, range(G))

@@ -19,7 +19,9 @@ ROWS = D // PACK
 RUN = 4
 N_PASS = 128
 CHUNKS = (slice(0, 256), slice(256, 384), slice(384, 512))
-STORE_COLS = 256
+Z_PLACE = ((0, 0), (0, 256), (1, 256))
+V_PLACE = ((1, 0), (0, 384), (0, 0))
+GROUPS_PER_STORE = (1, 2, 1)
 
 
 def width(cols):
@@ -61,8 +63,7 @@ def tile_rows_gglu_silu_kernel(tc, x, w, u, out):
         x_codes = sb.tile([P, N], U32, name="x_codes", align_bytes=64)
         x_scales = sb.tile([P, N], U8, name="x_scales", align_bytes=64)
         warm = sb.tile([P, 1], F32, name="warm")
-        z_ps = [ps.tile([M, N], F32, name="z_ps%d" % g) for g in range(G)]
-        v_ps = [ps.tile([M, N], F32, name="v_ps%d" % g) for g in range(G)]
+        banks = [[ps.tile([M, N], F32, name="bank%d_%d" % (b, g)) for g in range(G)] for b in range(2)]
         act = [sb.tile([M, G * width(cols)], F32, name="act%d" % c) for c, cols in enumerate(CHUNKS)]
         res = [sb.tile([M, G * width(cols)], F32, name="res%d" % c) for c, cols in enumerate(CHUNKS)]
 
@@ -79,13 +80,17 @@ def tile_rows_gglu_silu_kernel(tc, x, w, u, out):
         def quantize_x(c):
             quantize(x_codes[:, CHUNKS[c]], x_scales[:, CHUNKS[c]], x_bf[c][:])
 
-        def product(banks, codes, scales, c):
-            for n0 in range(CHUNKS[c].start, CHUNKS[c].stop, N_PASS):
-                cols = slice(n0, n0 + N_PASS)
-                for g in range(G):
+        def sums(place, c, g):
+            bank, first = place[c]
+            return banks[bank][g][:, first : first + width(CHUNKS[c])]
+
+        def product(place, codes, scales, c, groups):
+            for n0 in range(0, width(CHUNKS[c]), N_PASS):
+                cols = slice(CHUNKS[c].start + n0, CHUNKS[c].start + n0 + N_PASS)
+                for g in groups:
                     rows = slice(g * ROWS, (g + 1) * ROWS)
                     nc.tensor.matmul_mx(
-                        out=banks[g][:, cols],
+                        out=sums(place, c, g)[:, n0 : n0 + N_PASS],
                         lhsT=codes[rows, :].bitcast(FP8X4),
                         lhsT_scale=scales[rows, :],
                         rhs=x_codes[rows, cols].bitcast(FP8X4),
@@ -94,19 +99,25 @@ def tile_rows_gglu_silu_kernel(tc, x, w, u, out):
                         stop=True,
                     )
 
+        def z_product(c, groups):
+            product(Z_PLACE, w_codes, w_scales, c, groups)
+
+        def v_product(c, groups):
+            product(V_PLACE, u_codes, u_scales, c, groups)
+
         def group_cols(c, first, last):
             return slice(first * width(CHUNKS[c]), (last + 1) * width(CHUNKS[c]))
 
         def activate(c):
             for g in range(G):
-                nc.scalar.activation(out=act[c][:, group_cols(c, g, g)], in_=z_ps[g][:, CHUNKS[c]], func=SILU)
+                nc.scalar.activation(out=act[c][:, group_cols(c, g, g)], in_=sums(Z_PLACE, c, g), func=SILU)
 
         def gate_and_store(c, groups):
-            per_store = STORE_COLS // width(CHUNKS[c])
+            per_store = GROUPS_PER_STORE[c]
             for g in groups:
                 nc.vector.tensor_tensor(
                     out=res[c][:, group_cols(c, g, g)],
-                    in0=v_ps[g][:, CHUNKS[c]],
+                    in0=sums(V_PLACE, c, g),
                     in1=act[c][:, group_cols(c, g, g)],
                     op=MULT,
                 )
@@ -123,30 +134,33 @@ def tile_rows_gglu_silu_kernel(tc, x, w, u, out):
         load_x(1)
         load_x(2)
 
-        nc.scalar.activation(out=warm[:], in_=x_raw[0][:, 0, 0:1], func=SILU)
+        nc.vector.memset(warm[:], 0.0)
+        nc.scalar.activation(out=warm[:], in_=warm[:], func=SILU)
 
         interleave_shared(x_bf[0], x_raw[0], 160)
         interleave_shared(w_bf, w_raw, 80)
         quantize_x(0)
         quantize(w_codes[:], w_scales[:], w_bf[:])
-        product(z_ps, w_codes, w_scales, 0)
+        z_product(0, range(G))
         interleave_shared(u_bf, u_raw, 64)
         quantize(u_codes[:], u_scales[:], u_bf[:])
-        product(v_ps, u_codes, u_scales, 0)
-        activate(0)
+        v_product(0, range(G))
 
-        interleave(nc.vector.tensor_copy, x_bf[1], x_raw[1], 0, width(CHUNKS[1]))
-        gate_and_store(0, range(1))
+        interleave_shared(x_bf[1], x_raw[1], 64)
         quantize_x(1)
-        product(z_ps, w_codes, w_scales, 1)
-        interleave(nc.scalar.copy, x_bf[2], x_raw[2], 0, width(CHUNKS[2]))
-        gate_and_store(0, range(1, G))
-        product(v_ps, u_codes, u_scales, 1)
-        activate(1)
+        interleave(nc.vector.tensor_copy, x_bf[2], x_raw[2], 0, width(CHUNKS[2]))
 
+        activate(0)
+        for g in range(G):
+            z_product(1, [g])
+            v_product(1, [g])
+        gate_and_store(0, range(G - 1))
         quantize_x(2)
-        product(z_ps, w_codes, w_scales, 2)
+        gate_and_store(0, [G - 1])
+
+        activate(1)
+        z_product(2, range(G))
         gate_and_store(1, range(G))
-        product(v_ps, u_codes, u_scales, 2)
+        v_product(2, range(G))
         activate(2)
         gate_and_store(2, range(G))

from contextlib import ExitStack

import concourse.mybir as mybir

G, D, M, N = 4, 128, 128, 512
FLOPS = 2 * 2 * G * D * M * N

F32 = mybir.dt.float32
BF16 = mybir.dt.bfloat16
U32 = mybir.dt.uint32
U8 = mybir.dt.uint8
FP8X4 = mybir.dt.float8_e4m3fn_x4
SILU = mybir.ActivationFunctionType.Silu
MULT = mybir.AluOpType.mult

P = 128
PACK = 4
ROWS = D // PACK
RUN = 4
N_PASS = 128
CHUNKS = (slice(0, 256), slice(256, 384), slice(384, 512))
Z_PLACE = ((0, 0), (0, 256), (1, 256))
V_PLACE = ((1, 0), (0, 384), (0, 0))
GROUPS_PER_STORE = (1, 2, 1)


def width(cols):
    return cols.stop - cols.start


def interleave(copy, dst, src, lo, hi):
    copy(
        out=dst[:, PACK * lo : PACK * hi].rearrange("p (c i j) -> p c j i", i=RUN, j=PACK),
        in_=src[:, :, lo:hi].rearrange("p j (c i) -> p c j i", i=RUN),
    )


def tile_rows_gglu_silu_kernel(tc, x, w, u, out):
    nc = tc.nc
    x_rows = x.rearrange("g (p j) n -> (g p) j n", j=PACK)
    w_rows = w.rearrange("g (p j) m -> (g p) j m", j=PACK)
    u_rows = u.rearrange("g (p j) m -> (g p) j m", j=PACK)
    out_rows = out.rearrange("g m n -> m g n")

    with ExitStack() as ctx:
        sb = ctx.enter_context(tc.tile_pool(name="sb", bufs=1))
        ps = ctx.enter_context(tc.psum_pool(name="ps", bufs=1))
        ctx.enter_context(tc.manual_schedule())

        w_raw = sb.tile([P, PACK, M], F32, name="w_raw")
        u_raw = sb.tile([P, PACK, M], F32, name="u_raw")
        x_raw = [sb.tile([P, PACK, width(cols)], F32, name="x_raw%d" % c) for c, cols in enumerate(CHUNKS)]
        w_bf = sb.tile([P, PACK * M], BF16, name="w_bf", align_bytes=64)
        u_bf = sb.tile([P, PACK * M], BF16, name="u_bf", align_bytes=64)
        x_bf = [
            sb.tile([P, PACK * width(cols)], BF16, name="x_bf%d" % c, align_bytes=64)
            for c, cols in enumerate(CHUNKS)
        ]
        w_codes = sb.tile([P, M], U32, name="w_codes", align_bytes=64)
        w_scales = sb.tile([P, M], U8, name="w_scales", align_bytes=64)
        u_codes = sb.tile([P, M], U32, name="u_codes", align_bytes=64)
        u_scales = sb.tile([P, M], U8, name="u_scales", align_bytes=64)
        x_codes = sb.tile([P, N], U32, name="x_codes", align_bytes=64)
        x_scales = sb.tile([P, N], U8, name="x_scales", align_bytes=64)
        warm = sb.tile([P, 1], F32, name="warm")
        banks = [[ps.tile([M, N], F32, name="bank%d_%d" % (b, g)) for g in range(G)] for b in range(2)]
        act = [sb.tile([M, G * width(cols)], F32, name="act%d" % c) for c, cols in enumerate(CHUNKS)]
        res = [sb.tile([M, G * width(cols)], F32, name="res%d" % c) for c, cols in enumerate(CHUNKS)]

        def load_x(c):
            nc.sync.dma_start(out=x_raw[c][:], in_=x_rows[:, :, CHUNKS[c]])

        def interleave_shared(dst, src, vec_cols):
            interleave(nc.vector.tensor_copy, dst, src, 0, vec_cols)
            interleave(nc.scalar.copy, dst, src, vec_cols, src.shape[2])

        def quantize(codes, scales, src):
            nc.vector.quantize_mx(out=codes.bitcast(FP8X4), scales=scales, in_=src)

        def quantize_x(c):
            quantize(x_codes[:, CHUNKS[c]], x_scales[:, CHUNKS[c]], x_bf[c][:])

        def sums(place, c, g):
            bank, first = place[c]
            return banks[bank][g][:, first : first + width(CHUNKS[c])]

        def product(place, codes, scales, c, groups):
            for n0 in range(0, width(CHUNKS[c]), N_PASS):
                cols = slice(CHUNKS[c].start + n0, CHUNKS[c].start + n0 + N_PASS)
                for g in groups:
                    rows = slice(g * ROWS, (g + 1) * ROWS)
                    nc.tensor.matmul_mx(
                        out=sums(place, c, g)[:, n0 : n0 + N_PASS],
                        lhsT=codes[rows, :].bitcast(FP8X4),
                        lhsT_scale=scales[rows, :],
                        rhs=x_codes[rows, cols].bitcast(FP8X4),
                        rhs_scale=x_scales[rows, cols],
                        start=True,
                        stop=True,
                    )

        def z_product(c, groups):
            product(Z_PLACE, w_codes, w_scales, c, groups)

        def v_product(c, groups):
            product(V_PLACE, u_codes, u_scales, c, groups)

        def group_cols(c, first, last):
            return slice(first * width(CHUNKS[c]), (last + 1) * width(CHUNKS[c]))

        def activate(c):
            for g in range(G):
                nc.scalar.activation(out=act[c][:, group_cols(c, g, g)], in_=sums(Z_PLACE, c, g), func=SILU)

        def gate_and_store(c, groups):
            per_store = GROUPS_PER_STORE[c]
            for g in groups:
                nc.vector.tensor_tensor(
                    out=res[c][:, group_cols(c, g, g)],
                    in0=sums(V_PLACE, c, g),
                    in1=act[c][:, group_cols(c, g, g)],
                    op=MULT,
                )
                if (g + 1) % per_store == 0:
                    first = g + 1 - per_store
                    nc.sync.dma_start(
                        out=out_rows[:, first : g + 1, CHUNKS[c]],
                        in_=res[c][:, group_cols(c, first, g)].rearrange("m (g n) -> m g n", g=per_store),
                    )

        load_x(0)
        nc.sync.dma_start(out=w_raw[:], in_=w_rows)
        nc.sync.dma_start(out=u_raw[:], in_=u_rows)
        load_x(1)
        load_x(2)

        nc.vector.memset(warm[:], 0.0)
        nc.scalar.activation(out=warm[:], in_=warm[:], func=SILU)

        interleave_shared(x_bf[0], x_raw[0], 160)
        interleave_shared(w_bf, w_raw, 80)
        quantize_x(0)
        quantize(w_codes[:], w_scales[:], w_bf[:])
        z_product(0, range(G))
        interleave_shared(u_bf, u_raw, 64)
        quantize(u_codes[:], u_scales[:], u_bf[:])
        v_product(0, range(G))

        interleave_shared(x_bf[1], x_raw[1], 64)
        quantize_x(1)
        interleave(nc.vector.tensor_copy, x_bf[2], x_raw[2], 0, width(CHUNKS[2]))

        activate(0)
        for g in range(G):
            z_product(1, [g])
            v_product(1, [g])
        gate_and_store(0, range(G - 1))
        quantize_x(2)
        gate_and_store(0, [G - 1])

        activate(1)
        z_product(2, range(G))
        gate_and_store(1, range(G))
        v_product(2, range(G))
        activate(2)
        gate_and_store(2, range(G))
